import numpy as np
CORES = [0,4,8,12,16,20,24,28]
N = 8
def setup_inputs(rng):
    return {"x": rng.standard_normal((N, 128, 1024), dtype=np.float32)}
def reference(x):
    s = x.sum(axis=0, dtype=np.float64).astype(x.dtype)
    b = 1024 // N
    return {"y": np.stack([s[:, r * b:(r + 1) * b] for r in range(N)])}

@@ -1,0 +1,78 @@
+from concourse.bass import DstId, RemoteDMATransfer
+from concourse.mybir import AluOpType
+
+SCRATCH = {
+    "xb": ("dram", [16, 128, 64], "float32"),
+    "inb": ("dram", [8, 128, 64], "float32"),
+    "land_o": ("dram", [2, 128, 64], "float32"),
+    "land_s": ("dram", [2, 128, 64], "float32"),
+}
+SEMAPHORES = ["ld0", "ld1", "sent", "arr", "arr_o", "arr_s", "st", "acc"]
+
+
+def rank_program(g, core, T, topo):
+    chip, k = core // 8, core % 8
+    sem = T.sem
+
+    def dst_id(c):
+        rid, pid, _se = topo.addr(c)
+        return DstId(rid=rid, pnc=pid)
+
+    if k in (0, 4):
+        w = k // 4
+        plane, mate, far = chip ^ 2, chip ^ 1, chip ^ 3
+
+        def load(q, t, s):
+            q.dma_start(T.xb[2 * t:2 * t + 2], T.x[:, 128 * t:128 * t + 128]).then_inc(s, 16)
+
+        for s, chips in ((sem.ld0, (far, mate)), (sem.ld1, (plane, chip))):
+            for c in chips:
+                load(g.sync, 2 * c, s)
+                load(g.scalar, 2 * c + 1, s)
+
+        def call(pairs):
+            tr = []
+            for (dc, hc, base, split) in pairs:
+                off = 0 if hc != chip else 8
+                slot = w if hc == chip else 2 + w
+                for j in range(2):
+                    for h in range(2):
+                        helper = 8 * hc + base + 4 * j + (h if split else 0)
+                        tr.append(RemoteDMATransfer(
+                            dst_ids=[dst_id(helper)], dma_engine_mask=0x3 << (off + 4 * j + 2 * h),
+                            remote_sem=sem.arr, src=T.xb[2 * (2 * dc + j) + h],
+                            dst=T.inb[slot if split else 2 * slot + h]))
+            g.remote_dma_fused(tr, local_sem=sem.sent)
+
+        g.wait_ge(sem.ld0, 64)
+        call([(far, plane, 2, True), (mate, chip, 2, True)])
+        g.wait_ge(sem.ld1, 64)
+        call([(plane, plane, 1, False), (chip, chip, 1, False)])
+        g.wait_ge(sem.sent, 32)
+
+        g.sync.wait_ge(sem.arr_o, 16)
+        g.sync.dma_start(T.y[:, :], T.land_o[:]).then_inc(sem.st, 16)
+        g.wait_ge(sem.arr_s, 16)
+        g.wait_ge(sem.st, 16)
+        g.dma_start(T.y[:, :], T.land_s[:], accum_op=AluOpType.add, max_dma_last_dim=8192).then_inc(sem.acc, 16)
+        g.wait_ge(sem.acc, 16)
+        return
+
+    j = k // 4
+    if k % 4 == 1:
+        dst = dst_id(8 * chip + 4 * j)
+        g.wait_ge(sem.arr, 16)
+        g.remote_dma_fused([
+            RemoteDMATransfer(dst_ids=[dst], dma_engine_mask=0xFF << (8 * h), remote_sem=sem.arr_s,
+                              srcs=[T.inb[2 * s + h] for s in range(4)], dsts=[T.land_s[h]], alu_op=1)
+            for h in range(2)], local_sem=sem.sent)
+        g.wait_ge(sem.sent, 16)
+    else:
+        h = k % 4 - 2
+        dst = dst_id(8 * (chip ^ 1) + 4 * j)
+        g.wait_ge(sem.arr, 8)
+        g.remote_dma_fused([
+            RemoteDMATransfer(dst_ids=[dst], dma_engine_mask=0xFF, remote_sem=sem.arr_o,
+                              srcs=[T.inb[s] for s in range(4)], dsts=[T.land_o[h]], alu_op=1)],
+            local_sem=sem.sent)
+        g.wait_ge(sem.sent, 8)

@@ -7,7 +7,21 @@ SCRATCH = {
     "land_o": ("dram", [2, 128, 64], "float32"),
     "land_s": ("dram", [2, 128, 64], "float32"),
 }
-SEMAPHORES = ["ld0", "ld1", "sent", "arr", "arr_o", "arr_s", "st", "acc"]
+SEMAPHORES = ["ld0", "ld1", "ld2", "ld3", "sent", "arr", "arrf", "arr_o", "arr_s", "st", "acc"]
+
+STAGES = [["far", "mate"], ["plane", "own"]]
+STORE_FIRST = "o"
+OFFCHIP = ("far", "plane")
+F_CORE = (1, 3)
+
+
+def engines(grp):
+    for st in STAGES:
+        if grp in st:
+            kind = [x for x in st if (x in OFFCHIP) == (grp in OFFCHIP)]
+            e = 2 // len(kind)
+            return (0 if grp in OFFCHIP else 8) + 4 * e * kind.index(grp), e
+    return None
 
 
 def rank_program(g, core, T, topo):
@@ -20,59 +34,58 @@ def rank_program(g, core, T, topo):
 
     if k in (0, 4):
         w = k // 4
-        plane, mate, far = chip ^ 2, chip ^ 1, chip ^ 3
+        info = {"far": (chip ^ 3, chip ^ 2, True), "mate": (chip ^ 1, chip, True),
+                "plane": (chip ^ 2, chip ^ 2, False), "own": (chip, chip, False)}
 
-        def load(q, t, s):
-            q.dma_start(T.xb[2 * t:2 * t + 2], T.x[:, 128 * t:128 * t + 128]).then_inc(s, 16)
+        for i, st in enumerate(STAGES):
+            for grp in st:
+                for j, q in enumerate((g.sync, g.scalar)):
+                    t = 2 * info[grp][0] + j
+                    q.dma_start(T.xb[2 * t:2 * t + 2], T.x[:, 128 * t:128 * t + 128]).then_inc(sem["ld%d" % i], 16)
 
-        for s, chips in ((sem.ld0, (far, mate)), (sem.ld1, (plane, chip))):
-            for c in chips:
-                load(g.sync, 2 * c, s)
-                load(g.scalar, 2 * c + 1, s)
-
-        def call(pairs):
+        sent = 0
+        for i, st in enumerate(STAGES):
             tr = []
-            for (dc, hc, base, split) in pairs:
-                off = 0 if hc != chip else 8
+            for grp in st:
+                dc, hc, m_fold = info[grp]
+                e0, e = engines(grp)
                 slot = w if hc == chip else 2 + w
                 for j in range(2):
                     for h in range(2):
-                        helper = 8 * hc + base + 4 * j + (h if split else 0)
+                        helper = 8 * hc + 4 * j + (2 + h if m_fold else F_CORE[h])
                         tr.append(RemoteDMATransfer(
-                            dst_ids=[dst_id(helper)], dma_engine_mask=0x3 << (off + 4 * j + 2 * h),
-                            remote_sem=sem.arr, src=T.xb[2 * (2 * dc + j) + h],
-                            dst=T.inb[slot if split else 2 * slot + h]))
+                            dst_ids=[dst_id(helper)], dma_engine_mask=((1 << e) - 1) << (e0 + e * (2 * j + h)),
+                            remote_sem=sem.arr if m_fold else sem.arrf, src=T.xb[2 * (2 * dc + j) + h],
+                            dst=T.inb[slot if m_fold else 4 + slot]))
+                        sent += e
+            g.wait_ge(sem["ld%d" % i], 32 * len(st))
             g.remote_dma_fused(tr, local_sem=sem.sent)
+        g.wait_ge(sem.sent, sent)
 
-        g.wait_ge(sem.ld0, 64)
-        call([(far, plane, 2, True), (mate, chip, 2, True)])
-        g.wait_ge(sem.ld1, 64)
-        call([(plane, plane, 1, False), (chip, chip, 1, False)])
-        g.wait_ge(sem.sent, 32)
-
-        g.sync.wait_ge(sem.arr_o, 16)
-        g.sync.dma_start(T.y[:, :], T.land_o[:]).then_inc(sem.st, 16)
-        g.wait_ge(sem.arr_s, 16)
+        first, a_first, n_first, second, a_second, n_second = (T.land_o, sem.arr_o, 16, T.land_s, sem.arr_s, 32) \
+            if STORE_FIRST == "o" else (T.land_s, sem.arr_s, 32, T.land_o, sem.arr_o, 16)
+        g.sync.wait_ge(a_first, n_first)
+        g.sync.dma_start(T.y[:, :], first[:]).then_inc(sem.st, 16)
+        g.wait_ge(a_second, n_second)
         g.wait_ge(sem.st, 16)
-        g.dma_start(T.y[:, :], T.land_s[:], accum_op=AluOpType.add, max_dma_last_dim=8192).then_inc(sem.acc, 16)
+        g.dma_start(T.y[:, :], second[:], accum_op=AluOpType.add, max_dma_last_dim=8192).then_inc(sem.acc, 16)
         g.wait_ge(sem.acc, 16)
         return
 
-    j = k // 4
-    if k % 4 == 1:
-        dst = dst_id(8 * chip + 4 * j)
-        g.wait_ge(sem.arr, 16)
+    j, kk = k // 4, k % 4
+    sent = 0
+    if kk >= 2:
+        g.wait_ge(sem.arr, 2 * (engines("far")[1] + engines("mate")[1]))
         g.remote_dma_fused([
-            RemoteDMATransfer(dst_ids=[dst], dma_engine_mask=0xFF << (8 * h), remote_sem=sem.arr_s,
-                              srcs=[T.inb[2 * s + h] for s in range(4)], dsts=[T.land_s[h]], alu_op=1)
-            for h in range(2)], local_sem=sem.sent)
-        g.wait_ge(sem.sent, 16)
-    else:
-        h = k % 4 - 2
-        dst = dst_id(8 * (chip ^ 1) + 4 * j)
-        g.wait_ge(sem.arr, 8)
-        g.remote_dma_fused([
-            RemoteDMATransfer(dst_ids=[dst], dma_engine_mask=0xFF, remote_sem=sem.arr_o,
-                              srcs=[T.inb[s] for s in range(4)], dsts=[T.land_o[h]], alu_op=1)],
+            RemoteDMATransfer(dst_ids=[dst_id(8 * (chip ^ 1) + 4 * j)], dma_engine_mask=0xFF, remote_sem=sem.arr_o,
+                              srcs=[T.inb[s] for s in range(4)], dsts=[T.land_o[kk - 2]], alu_op=1)],
             local_sem=sem.sent)
-        g.wait_ge(sem.sent, 8)
+        sent += 8
+    if kk in F_CORE:
+        g.wait_ge(sem.arrf, 2 * (engines("plane")[1] + engines("own")[1]))
+        g.remote_dma_fused([
+            RemoteDMATransfer(dst_ids=[dst_id(8 * chip + 4 * j)], dma_engine_mask=0xFFFF, remote_sem=sem.arr_s,
+                              srcs=[T.inb[4 + s] for s in range(4)], dsts=[T.land_s[F_CORE.index(kk)]], alu_op=1)],
+            local_sem=sem.sent)
+        sent += 16
+    g.wait_ge(sem.sent, sent)

@@ -3,7 +3,7 @@ from concourse.mybir import AluOpType
 
 SCRATCH = {
     "xb": ("dram", [16, 128, 64], "float32"),
-    "inb": ("dram", [8, 128, 64], "float32"),
+    "inb": ("dram", [9, 128, 64], "float32"),
     "land_o": ("dram", [2, 128, 64], "float32"),
     "land_s": ("dram", [2, 128, 64], "float32"),
 }
@@ -13,6 +13,7 @@ STAGES = [["far", "mate"], ["plane", "own"]]
 STORE_FIRST = "o"
 OFFCHIP = ("far", "plane")
 F_CORE = (1, 3)
+FIVE = True
 
 
 def engines(grp):
@@ -62,6 +63,11 @@ def rank_program(g, core, T, topo):
             g.remote_dma_fused(tr, local_sem=sem.sent)
         g.wait_ge(sem.sent, sent)
 
+        if FIVE:
+            g.sync.wait_ge(sem.arr_s, 32)
+            g.sync.dma_start(T.y[:, :], T.land_s[:]).then_inc(sem.st, 16)
+            g.wait_ge(sem.st, 16)
+            return
         first, a_first, n_first, second, a_second, n_second = (T.land_o, sem.arr_o, 16, T.land_s, sem.arr_s, 32) \
             if STORE_FIRST == "o" else (T.land_s, sem.arr_s, 32, T.land_o, sem.arr_o, 16)
         g.sync.wait_ge(a_first, n_first)
@@ -75,17 +81,20 @@ def rank_program(g, core, T, topo):
     j, kk = k // 4, k % 4
     sent = 0
     if kk >= 2:
+        h = kk - 2
         g.wait_ge(sem.arr, 2 * (engines("far")[1] + engines("mate")[1]))
         g.remote_dma_fused([
-            RemoteDMATransfer(dst_ids=[dst_id(8 * (chip ^ 1) + 4 * j)], dma_engine_mask=0xFF, remote_sem=sem.arr_o,
-                              srcs=[T.inb[s] for s in range(4)], dsts=[T.land_o[kk - 2]], alu_op=1)],
+            RemoteDMATransfer(dst_ids=[dst_id(8 * (chip ^ 1) + 4 * j + (F_CORE[h] if FIVE else 0))],
+                              dma_engine_mask=0xFF, remote_sem=sem.arrf if FIVE else sem.arr_o,
+                              srcs=[T.inb[s] for s in range(4)], dsts=[T.inb[8] if FIVE else T.land_o[h]], alu_op=1)],
             local_sem=sem.sent)
         sent += 8
     if kk in F_CORE:
-        g.wait_ge(sem.arrf, 2 * (engines("plane")[1] + engines("own")[1]))
+        g.wait_ge(sem.arrf, 2 * (engines("plane")[1] + engines("own")[1]) + (8 if FIVE else 0))
         g.remote_dma_fused([
             RemoteDMATransfer(dst_ids=[dst_id(8 * chip + 4 * j)], dma_engine_mask=0xFFFF, remote_sem=sem.arr_s,
-                              srcs=[T.inb[4 + s] for s in range(4)], dsts=[T.land_s[F_CORE.index(kk)]], alu_op=1)],
+                              srcs=[T.inb[4 + s] for s in range(5 if FIVE else 4)],
+                              dsts=[T.land_s[F_CORE.index(kk)]], alu_op=1)],
             local_sem=sem.sent)
         sent += 16
     g.wait_ge(sem.sent, sent)

@@ -1,28 +1,16 @@
 from concourse.bass import DstId, RemoteDMATransfer
-from concourse.mybir import AluOpType
 
 SCRATCH = {
     "xb": ("dram", [16, 128, 64], "float32"),
     "inb": ("dram", [9, 128, 64], "float32"),
-    "land_o": ("dram", [2, 128, 64], "float32"),
-    "land_s": ("dram", [2, 128, 64], "float32"),
+    "land": ("dram", [2, 128, 64], "float32"),
 }
-SEMAPHORES = ["ld0", "ld1", "ld2", "ld3", "sent", "arr", "arrf", "arr_o", "arr_s", "st", "acc"]
+SEMAPHORES = ["ld0", "ld1", "sent", "arr", "arrf", "done", "st"]
 
 STAGES = [["far", "mate"], ["plane", "own"]]
-STORE_FIRST = "o"
 OFFCHIP = ("far", "plane")
 F_CORE = (1, 3)
-FIVE = True
-
-
-def engines(grp):
-    for st in STAGES:
-        if grp in st:
-            kind = [x for x in st if (x in OFFCHIP) == (grp in OFFCHIP)]
-            e = 2 // len(kind)
-            return (0 if grp in OFFCHIP else 8) + 4 * e * kind.index(grp), e
-    return None
+E = 2
 
 
 def rank_program(g, core, T, topo):
@@ -49,52 +37,40 @@ def rank_program(g, core, T, topo):
             tr = []
             for grp in st:
                 dc, hc, m_fold = info[grp]
-                e0, e = engines(grp)
+                e0 = 0 if grp in OFFCHIP else 8
                 slot = w if hc == chip else 2 + w
                 for j in range(2):
                     for h in range(2):
                         helper = 8 * hc + 4 * j + (2 + h if m_fold else F_CORE[h])
                         tr.append(RemoteDMATransfer(
-                            dst_ids=[dst_id(helper)], dma_engine_mask=((1 << e) - 1) << (e0 + e * (2 * j + h)),
+                            dst_ids=[dst_id(helper)], dma_engine_mask=((1 << E) - 1) << (e0 + E * (2 * j + h)),
                             remote_sem=sem.arr if m_fold else sem.arrf, src=T.xb[2 * (2 * dc + j) + h],
                             dst=T.inb[slot if m_fold else 4 + slot]))
-                        sent += e
+                        sent += E
             g.wait_ge(sem["ld%d" % i], 32 * len(st))
             g.remote_dma_fused(tr, local_sem=sem.sent)
         g.wait_ge(sem.sent, sent)
 
-        if FIVE:
-            g.sync.wait_ge(sem.arr_s, 32)
-            g.sync.dma_start(T.y[:, :], T.land_s[:]).then_inc(sem.st, 16)
-            g.wait_ge(sem.st, 16)
-            return
-        first, a_first, n_first, second, a_second, n_second = (T.land_o, sem.arr_o, 16, T.land_s, sem.arr_s, 32) \
-            if STORE_FIRST == "o" else (T.land_s, sem.arr_s, 32, T.land_o, sem.arr_o, 16)
-        g.sync.wait_ge(a_first, n_first)
-        g.sync.dma_start(T.y[:, :], first[:]).then_inc(sem.st, 16)
-        g.wait_ge(a_second, n_second)
+        g.sync.wait_ge(sem.done, 32)
+        g.sync.dma_start(T.y[:, :], T.land[:]).then_inc(sem.st, 16)
         g.wait_ge(sem.st, 16)
-        g.dma_start(T.y[:, :], second[:], accum_op=AluOpType.add, max_dma_last_dim=8192).then_inc(sem.acc, 16)
-        g.wait_ge(sem.acc, 16)
         return
 
     j, kk = k // 4, k % 4
     sent = 0
     if kk >= 2:
-        h = kk - 2
-        g.wait_ge(sem.arr, 2 * (engines("far")[1] + engines("mate")[1]))
+        g.wait_ge(sem.arr, 4 * E)
         g.remote_dma_fused([
-            RemoteDMATransfer(dst_ids=[dst_id(8 * (chip ^ 1) + 4 * j + (F_CORE[h] if FIVE else 0))],
-                              dma_engine_mask=0xFF, remote_sem=sem.arrf if FIVE else sem.arr_o,
-                              srcs=[T.inb[s] for s in range(4)], dsts=[T.inb[8] if FIVE else T.land_o[h]], alu_op=1)],
+            RemoteDMATransfer(dst_ids=[dst_id(8 * (chip ^ 1) + 4 * j + F_CORE[kk - 2])],
+                              dma_engine_mask=0xFF, remote_sem=sem.arrf,
+                              srcs=[T.inb[s] for s in range(4)], dsts=[T.inb[8]], alu_op=1)],
             local_sem=sem.sent)
         sent += 8
     if kk in F_CORE:
-        g.wait_ge(sem.arrf, 2 * (engines("plane")[1] + engines("own")[1]) + (8 if FIVE else 0))
+        g.wait_ge(sem.arrf, 4 * E + 8)
         g.remote_dma_fused([
-            RemoteDMATransfer(dst_ids=[dst_id(8 * chip + 4 * j)], dma_engine_mask=0xFFFF, remote_sem=sem.arr_s,
-                              srcs=[T.inb[4 + s] for s in range(5 if FIVE else 4)],
-                              dsts=[T.land_s[F_CORE.index(kk)]], alu_op=1)],
+            RemoteDMATransfer(dst_ids=[dst_id(8 * chip + 4 * j)], dma_engine_mask=0xFFFF, remote_sem=sem.done,
+                              srcs=[T.inb[4 + s] for s in range(5)], dsts=[T.land[F_CORE.index(kk)]], alu_op=1)],
             local_sem=sem.sent)
         sent += 16
     g.wait_ge(sem.sent, sent)

from concourse.bass import DstId, RemoteDMATransfer

SCRATCH = {
    "xb": ("dram", [16, 128, 64], "float32"),
    "inb": ("dram", [9, 128, 64], "float32"),
    "land": ("dram", [2, 128, 64], "float32"),
}
SEMAPHORES = ["ld0", "ld1", "sent", "arr", "arrf", "done", "st"]

STAGES = [["far", "mate"], ["plane", "own"]]
OFFCHIP = ("far", "plane")
F_CORE = (1, 3)
E = 2


def rank_program(g, core, T, topo):
    chip, k = core // 8, core % 8
    sem = T.sem

    def dst_id(c):
        rid, pid, _se = topo.addr(c)
        return DstId(rid=rid, pnc=pid)

    if k in (0, 4):
        w = k // 4
        info = {"far": (chip ^ 3, chip ^ 2, True), "mate": (chip ^ 1, chip, True),
                "plane": (chip ^ 2, chip ^ 2, False), "own": (chip, chip, False)}

        for i, st in enumerate(STAGES):
            for grp in st:
                for j, q in enumerate((g.sync, g.scalar)):
                    t = 2 * info[grp][0] + j
                    q.dma_start(T.xb[2 * t:2 * t + 2], T.x[:, 128 * t:128 * t + 128]).then_inc(sem["ld%d" % i], 16)

        sent = 0
        for i, st in enumerate(STAGES):
            tr = []
            for grp in st:
                dc, hc, m_fold = info[grp]
                e0 = 0 if grp in OFFCHIP else 8
                slot = w if hc == chip else 2 + w
                for j in range(2):
                    for h in range(2):
                        helper = 8 * hc + 4 * j + (2 + h if m_fold else F_CORE[h])
                        tr.append(RemoteDMATransfer(
                            dst_ids=[dst_id(helper)], dma_engine_mask=((1 << E) - 1) << (e0 + E * (2 * j + h)),
                            remote_sem=sem.arr if m_fold else sem.arrf, src=T.xb[2 * (2 * dc + j) + h],
                            dst=T.inb[slot if m_fold else 4 + slot]))
                        sent += E
            g.wait_ge(sem["ld%d" % i], 32 * len(st))
            g.remote_dma_fused(tr, local_sem=sem.sent)
        g.wait_ge(sem.sent, sent)

        g.sync.wait_ge(sem.done, 32)
        g.sync.dma_start(T.y[:, :], T.land[:]).then_inc(sem.st, 16)
        g.wait_ge(sem.st, 16)
        return

    j, kk = k // 4, k % 4
    sent = 0
    if kk >= 2:
        g.wait_ge(sem.arr, 4 * E)
        g.remote_dma_fused([
            RemoteDMATransfer(dst_ids=[dst_id(8 * (chip ^ 1) + 4 * j + F_CORE[kk - 2])],
                              dma_engine_mask=0xFF, remote_sem=sem.arrf,
                              srcs=[T.inb[s] for s in range(4)], dsts=[T.inb[8]], alu_op=1)],
            local_sem=sem.sent)
        sent += 8
    if kk in F_CORE:
        g.wait_ge(sem.arrf, 4 * E + 8)
        g.remote_dma_fused([
            RemoteDMATransfer(dst_ids=[dst_id(8 * chip + 4 * j)], dma_engine_mask=0xFFFF, remote_sem=sem.done,
                              srcs=[T.inb[4 + s] for s in range(5)], dsts=[T.land[F_CORE.index(kk)]], alu_op=1)],
            local_sem=sem.sent)
        sent += 16
    g.wait_ge(sem.sent, sent)
